import numpy as np
import ml_dtypes


def mxq(x, axis, fmt="e4m3"):
    dtype, down = {"e4m3": (ml_dtypes.float8_e4m3fn, 7), "e5m2": (ml_dtypes.float8_e5m2, 14)}[fmt]
    v = np.moveaxis(np.asarray(x, np.float32).astype(ml_dtypes.bfloat16).astype(np.float64), axis, -1)
    blocks = v.reshape(v.shape[:-1] + (-1, 32))
    amax = np.abs(blocks).max(-1, keepdims=True)
    byte = np.maximum(np.where(amax > 0, np.frexp(amax)[1] - 1 + 127, 0) - down, 1)
    scale = np.exp2(byte - 127.0)
    codes = (blocks / scale).astype(np.float32).astype(dtype).astype(np.float64)
    return np.moveaxis((codes * scale).reshape(v.shape), -1, axis)


WIDE = False


def mx_kscale(k):
    if not WIDE:
        return np.ones(k)
    levels = np.array([10, -10, 5, -5, 0])
    if k % 512:
        return np.exp2(np.random.permutation(np.resize(levels, k // 32))).repeat(32)
    a = np.empty((k // 512, 16))
    for p in range(k // 512):
        a[p, :8] = np.random.permutation(np.resize(levels, 8))
        for g in range(8):
            far = levels[np.abs(levels - a[p, g]) >= 10]
            a[p, g + 8] = far[np.random.randint(len(far))]
    return np.exp2(a.ravel()).repeat(32)


def f64(x):
    return np.asarray(x).astype(np.float64)


def striped(idx):
    return np.tile(idx.reshape(-1, 16).T, (8, 1)).astype(np.uint16)


def unstriped(offs):
    return offs[:16].T.reshape(-1).astype(np.int64)


def pack_weight(w):
    k, n = w.shape
    w = f64(np.asarray(w, np.float32).astype(ml_dtypes.bfloat16)).reshape(k // 32, 32, n)
    amax = np.abs(w).max(1)
    byte = np.clip(np.where(amax > 0, np.frexp(amax)[1] - 1 + 127 - 7, 1), 1, 254)
    scaled = (w * np.exp2(127.0 - byte)[:, None, :]).reshape(k, n).astype(np.float32)
    words = np.ascontiguousarray(scaled.reshape(k // 512, 128, 4, n).transpose(0, 1, 3, 2)).astype(ml_dtypes.float8_e4m3fn).view(np.uint8)
    return words, np.ascontiguousarray(byte.astype(np.uint8).reshape(k // 512, 16, n))


def unpack_weight(words, scales):
    g, p, n, _ = words.shape
    vals = np.ascontiguousarray(words).view(ml_dtypes.float8_e4m3fn).astype(np.float64) * np.repeat(np.exp2(scales.astype(np.float64) - 127.0), 8, axis=1)[..., None]
    return vals.transpose(0, 1, 3, 2).reshape(g * 512, n)


def silu(v):
    return v / (1.0 + np.exp(-np.maximum(v, -700.0)))


K, T, E, C, N = 2048, 768, 12, 128, 256


def by_expert(wq, xq):
    return np.concatenate([wq[e].T @ xq[:, e * C:(e + 1) * C] for e in range(E)], axis=1)


def setup_inputs():
    n = np.random.standard_normal
    s = mx_kscale(K)[:, None]
    first = np.random.permutation(np.repeat(np.arange(E), T // E))
    second = (first + 1 + np.random.permutation(np.repeat(np.arange(E - 1), -(-T // (E - 1)))[:T])) % E
    while np.bincount(second, minlength=E).max() != T // E:
        load = np.bincount(second, minlength=E); hi, lo = int(load.argmax()), int(load.argmin())
        t = np.flatnonzero((second == hi) & (first != lo))[0]; second[t] = lo
    slot_token = np.empty(E * C, np.int64); pos = np.empty((2, T), np.int64); fill = np.zeros(E, np.int64)
    place = np.stack([np.random.permutation(C) for _ in range(E)])
    for r, deal in enumerate((first, second)):
        for t in np.random.permutation(T):
            e = deal[t]; j = e * C + place[e, fill[e]]; fill[e] += 1; slot_token[j] = t; pos[r, t] = j
    g = np.random.uniform(0.2, 0.8, T)
    packed = [pack_weight(m) for m in n((E, K, N)) / np.sqrt(K) / s[None]]
    return {
        "xT": (n((K, T)) * s).astype(np.float32),
        "w_words": np.stack([m[0] for m in packed]),
        "w_scales": np.stack([m[1] for m in packed]),
        "b": (0.3 * n((N, E))).astype(np.float32),
        "gate": np.stack([np.tile(g, (N, 1)), np.tile(1.0 - g, (N, 1))]).astype(np.float32),
        "offs": striped(slot_token),
        "pos1": striped(pos[0]),
        "pos2": striped(pos[1]),
    }


def reference(xT, w_words, w_scales, b, gate, offs, pos1, pos2):
    idx = unstriped(offs)
    xq = mxq(f64(xT)[:, idx], 0, "e4m3")
    w = np.stack([unpack_weight(w_words[e], w_scales[e]) for e in range(E)])
    y = by_expert(w, xq)
    y = silu(y + np.repeat(f64(b), C, axis=1))
    return f64(gate[0]) * y[:, unstriped(pos1)] + f64(gate[1]) * y[:, unstriped(pos2)]

@@ -1,0 +1,161 @@
+from contextlib import ExitStack
+
+import concourse.mybir as mybir
+
+K, T, E, C, N = 2048, 768, 12, 128, 256
+FLOPS = 2 * K * N * E * C
+
+F32 = mybir.dt.float32
+BF16 = mybir.dt.bfloat16
+U32 = mybir.dt.uint32
+I32 = mybir.dt.int32
+U16 = mybir.dt.uint16
+U8 = mybir.dt.uint8
+FP8X4 = mybir.dt.float8_e4m3fn_x4
+SILU = mybir.ActivationFunctionType.Silu
+MULT = mybir.AluOpType.mult
+
+P = 128
+PASSES = K // 512
+HALVES = N // P
+WIDE = 2048
+GROUPS = ((0, 4), (4, 8), (8, 10), (10, 12))
+BANKS = 4
+CHUNKS = ((0, 512), (512, 768))
+
+
+def tile_routed_moe_kernel(tc, xT, w_words, w_scales, b, gate, offs, pos1, pos2, out):
+    nc = tc.nc
+    with ExitStack() as ctx:
+        keep = ctx.enter_context(tc.tile_pool(name="keep", bufs=1))
+        psum = ctx.enter_context(tc.psum_pool(name="psum", bufs=1))
+
+        lists = keep.tile([P, E * C // 16], U16, name="lists")
+        p1 = keep.tile([P, T // 16], U16, name="p1")
+        p2 = keep.tile([P, T // 16], U16, name="p2")
+        bias = keep.tile([P, HALVES, E], F32, name="bias")
+        warm = keep.tile([P, 8], F32, name="warm")
+        raw = [keep.tile([P, 4, T], F32, name=f"raw{a}") for a in range(PASSES)]
+        pairs = [[keep.tile([P, c1 - c0, 4], BF16, name=f"pairs{a}_{c0}", align_bytes=64) for c0, c1 in CHUNKS] for a in range(PASSES)]
+        words = [keep.tile([P, WIDE if a < PASSES - 1 else T], I32, name=f"words{a}", align_bytes=64) for a in range(PASSES)]
+        scales = keep.tile([P, T], U8, name="scales", align_bytes=64)
+        g_words = [keep.tile([P, E * C], U32, name=f"g_words{a}", align_bytes=64) for a in range(PASSES)]
+        g_scales = keep.tile([P, E * C], U8, name="g_scales", align_bytes=64)
+        w = [[keep.tile([P, (e1 - e0) * PASSES, P], I32, name=f"w{h}_{e0}", align_bytes=64) for e0, e1 in GROUPS] for h in range(HALVES)]
+        w_sc = keep.tile([P, E * PASSES, N // 4], I32, name="w_sc", align_bytes=64)
+        y = [keep.tile([P, E * C], F32, name=f"y{h}") for h in range(HALVES)]
+        g = [[keep.tile([P, T], F32, name=f"g{h}_{r}") for r in range(2)] for h in range(HALVES)]
+        t = [[keep.tile([P, T], F32, name=f"t{h}_{r}") for r in range(2)] for h in range(HALVES)]
+        res = [keep.tile([P, T], F32, name=f"res{h}") for h in range(HALVES)]
+        banks = [[psum.tile([P, 512], F32, name=f"bank{h}_{j}") for j in range(BANKS)] for h in range(HALVES)]
+
+        nc.gpsimd.memset(scales[:], 0)
+        nc.vector.memset(warm[:], 0.0)
+        for a in range(PASSES - 1):
+            nc.vector.memset(words[a][:, T:WIDE], 0)
+        nc.gpsimd.memset(w_sc[:], 0)
+        nc.scalar.activation(warm[:], warm[:], SILU)
+
+        x_rows = xT.rearrange("(a p t) n -> a p t n", p=P, t=4)
+        nc.sync.dma_start(out=raw[0][:, :, 0:512], in_=x_rows[0, :, :, 0:512])
+        nc.sync.dma_start(out=raw[0][:, :, 512:T], in_=x_rows[0, :, :, 512:T])
+        nc.sync.dma_start(lists[:], offs)
+        for a in range(1, PASSES):
+            for c0, c1 in CHUNKS:
+                nc.sync.dma_start(out=raw[a][:, :, c0:c1], in_=x_rows[a, :, :, c0:c1])
+        ws_rows = w_scales.rearrange("e a (q i) n -> i q (e a) n", i=4)
+        for i in range(4):
+            nc.sync.dma_start(out=w_sc[i:P:32], in_=ws_rows[i].bitcast(I32))
+        w_rows = w_words.rearrange("e a p n r -> p (e a) (n r)")
+
+        def load_half(h):
+            for s, (e0, e1) in enumerate(GROUPS):
+                nc.sync.dma_start(
+                    out=w[h][s][:],
+                    in_=w_rows[:, e0 * PASSES : e1 * PASSES, h * 512 : (h + 1) * 512].bitcast(I32),
+                )
+            for r in range(2):
+                nc.sync.dma_start(out=g[h][r][:], in_=gate[r, h * P : (h + 1) * P, :])
+
+        load_half(0)
+        nc.sync.dma_start(p1[:], pos1)
+        nc.sync.dma_start(p2[:], pos2)
+        load_half(1)
+        nc.scalar.dma_start(out=bias[:], in_=b.rearrange("(h p) e -> p h e", p=P))
+
+        def cast(a, c0, c1, copy):
+            j = 0 if c0 < 512 else 1
+            base = CHUNKS[j][0]
+            copy(
+                out=pairs[a][j][:, c0 - base : c1 - base, :].rearrange("p (c i) t -> p c t i", i=4),
+                in_=raw[a][:, :, c0:c1].rearrange("p t (c i) -> p c t i", i=4),
+            )
+
+        def quantise(a):
+            for j, (c0, c1) in enumerate(CHUNKS):
+                nc.vector.quantize_mx(
+                    out=words[a][:, c0:c1].bitcast(FP8X4),
+                    scales=scales[4 * a : P, c0:c1],
+                    in_=pairs[a][j][:].rearrange("p c t -> p (c t)"),
+                )
+
+        def gather_words(a, e0, e1):
+            nc.vector.tensor_copy(
+                g_words[a][:, e0 * C : e1 * C],
+                words[a][:].bitcast(U32).indirect(lists[:, e0 * C // 16 : e1 * C // 16]),
+            )
+
+        def gather_scales(e0, e1):
+            nc.vector.tensor_copy(g_scales[:, e0 * C : e1 * C], scales[:].indirect(lists[:, e0 * C // 16 : e1 * C // 16]))
+
+        def multiply(h, s):
+            e0, e1 = GROUPS[s]
+            for e in range(e0, e1):
+                acc = banks[h][e % BANKS][:, e // BANKS * C : (e // BANKS + 1) * C]
+                slots = slice(e * C, (e + 1) * C)
+                for a in range(PASSES):
+                    nc.tensor.matmul_mx(
+                        out=acc,
+                        lhsT=w[h][s][:, (e - e0) * PASSES + a, :].bitcast(FP8X4),
+                        lhsT_scale=w_sc[:, e * PASSES + a, h * 32 : (h + 1) * 32].bitcast(U8),
+                        rhs=g_words[a][:, slots].bitcast(FP8X4),
+                        rhs_scale=g_scales[4 * a : P, slots],
+                        start=(a == 0),
+                        stop=(a == PASSES - 1),
+                    )
+                nc.scalar.activation(y[h][:, slots], acc, SILU, bias=bias[:, h, e : e + 1])
+
+        for c0, c1 in ((0, 256), (512, 640)):
+            cast(0, c0, c1, nc.vector.tensor_copy)
+        for c0, c1 in ((256, 512), (640, T)):
+            cast(0, c0, c1, nc.scalar.copy)
+        cast(1, 0, 512, nc.scalar.copy)
+        cast(1, 512, T, nc.vector.tensor_copy)
+        cast(2, 0, 512, nc.scalar.copy)
+        cast(2, 512, 640, nc.vector.tensor_copy)
+        cast(2, 640, T, nc.scalar.copy)
+        cast(3, 0, 512, nc.scalar.copy)
+        cast(3, 512, T, nc.scalar.copy)
+
+        for a in range(PASSES - 1):
+            quantise(a)
+            gather_words(a, 0, E)
+        quantise(PASSES - 1)
+        for s, (e0, e1) in enumerate(GROUPS):
+            gather_scales(e0, e1)
+            gather_words(PASSES - 1, e0, e1)
+            multiply(0, s)
+        for s in range(len(GROUPS)):
+            multiply(1, s)
+
+        def combine(h, c0, c1):
+            for r, p in ((0, p1), (1, p2)):
+                nc.vector.tensor_tensor(
+                    t[h][r][:, c0:c1], y[h][:].indirect(p[:, c0 // 16 : c1 // 16]), g[h][r][:, c0:c1], MULT
+                )
+            nc.vector.tensor_add(res[h][:, c0:c1], t[h][0][:, c0:c1], t[h][1][:, c0:c1])
+            nc.sync.dma_start(out=out[h * P : (h + 1) * P, c0:c1], in_=res[h][:, c0:c1])
+
+        combine(0, 0, T)
+        combine(1, 0, 512)
+        combine(1, 512, T)

@@ -1,6 +1,7 @@
 from contextlib import ExitStack
 
 import concourse.mybir as mybir
+from concourse.masks import make_identity
 
 K, T, E, C, N = 2048, 768, 12, 128, 256
 FLOPS = 2 * K * N * E * C
@@ -41,7 +42,7 @@ def tile_routed_moe_kernel(tc, xT, w_words, w_scales, b, gate, offs, pos1, pos2,
         scales = keep.tile([P, T], U8, name="scales", align_bytes=64)
         g_words = [keep.tile([P, E * C], U32, name=f"g_words{a}", align_bytes=64) for a in range(PASSES)]
         g_scales = keep.tile([P, E * C], U8, name="g_scales", align_bytes=64)
-        w = [[keep.tile([P, (e1 - e0) * PASSES, P], I32, name=f"w{h}_{e0}", align_bytes=64) for e0, e1 in GROUPS] for h in range(HALVES)]
+        w = [keep.tile([P, 2 * PASSES, N], I32, name=f"w{v}", align_bytes=64) for v in range(E // 2)]
         w_sc = keep.tile([P, E * PASSES, N // 4], I32, name="w_sc", align_bytes=64)
         y = [keep.tile([P, E * C], F32, name=f"y{h}") for h in range(HALVES)]
         g = [[keep.tile([P, T], F32, name=f"g{h}_{r}") for r in range(2)] for h in range(HALVES)]
@@ -49,38 +50,44 @@ def tile_routed_moe_kernel(tc, xT, w_words, w_scales, b, gate, offs, pos1, pos2,
         res = [keep.tile([P, T], F32, name=f"res{h}") for h in range(HALVES)]
         banks = [[psum.tile([P, 512], F32, name=f"bank{h}_{j}") for j in range(BANKS)] for h in range(HALVES)]
 
+        ident = keep.tile([P, P], F32, name="ident")
         nc.gpsimd.memset(scales[:], 0)
+        make_identity(nc, ident[:])
         nc.vector.memset(warm[:], 0.0)
+        nc.vector.memset(w_sc[:], 0)
         for a in range(PASSES - 1):
             nc.vector.memset(words[a][:, T:WIDE], 0)
-        nc.gpsimd.memset(w_sc[:], 0)
         nc.scalar.activation(warm[:], warm[:], SILU)
 
         x_rows = xT.rearrange("(a p t) n -> a p t n", p=P, t=4)
         nc.sync.dma_start(out=raw[0][:, :, 0:512], in_=x_rows[0, :, :, 0:512])
         nc.sync.dma_start(out=raw[0][:, :, 512:T], in_=x_rows[0, :, :, 512:T])
         nc.sync.dma_start(lists[:], offs)
-        for a in range(1, PASSES):
-            for c0, c1 in CHUNKS:
-                nc.sync.dma_start(out=raw[a][:, :, c0:c1], in_=x_rows[a, :, :, c0:c1])
-        ws_rows = w_scales.rearrange("e a (q i) n -> i q (e a) n", i=4)
-        for i in range(4):
-            nc.sync.dma_start(out=w_sc[i:P:32], in_=ws_rows[i].bitcast(I32))
+        ws_rows = w_scales.rearrange("e a q n -> q (e a) n")
         w_rows = w_words.rearrange("e a p n r -> p (e a) (n r)")
 
-        def load_half(h):
-            for s, (e0, e1) in enumerate(GROUPS):
-                nc.sync.dma_start(
-                    out=w[h][s][:],
-                    in_=w_rows[:, e0 * PASSES : e1 * PASSES, h * 512 : (h + 1) * 512].bitcast(I32),
-                )
-            for r in range(2):
-                nc.sync.dma_start(out=g[h][r][:], in_=gate[r, h * P : (h + 1) * P, :])
+        def load_w_scales(q0, q1):
+            for q in range(q0, q1):
+                row = q // 4 * 32 + q % 4
+                nc.sync.dma_start(out=w_sc[row : row + 1], in_=ws_rows[q : q + 1].bitcast(I32))
 
-        load_half(0)
+        def load_w(v):
+            nc.sync.dma_start(out=w[v][:], in_=w_rows[:, v * 2 * PASSES : (v + 1) * 2 * PASSES, :].bitcast(I32))
+
+        for c0, c1 in CHUNKS:
+            nc.sync.dma_start(out=raw[1][:, :, c0:c1], in_=x_rows[1, :, :, c0:c1])
+        load_w_scales(0, 2)
+        nc.sync.dma_start(out=raw[2][:], in_=x_rows[2])
+        load_w_scales(2, 4)
+        nc.sync.dma_start(out=raw[3][:], in_=x_rows[3])
+        for v in range(E // 2):
+            load_w_scales(4 + 3 * v, min(7 + 3 * v, 16))
+            load_w(v)
         nc.sync.dma_start(p1[:], pos1)
         nc.sync.dma_start(p2[:], pos2)
-        load_half(1)
+        for h in range(HALVES):
+            for r in range(2):
+                nc.sync.dma_start(out=g[h][r][:], in_=gate[r, h * P : (h + 1) * P, :])
         nc.scalar.dma_start(out=bias[:], in_=b.rearrange("(h p) e -> p h e", p=P))
 
         def cast(a, c0, c1, copy):
@@ -116,7 +123,7 @@ def tile_routed_moe_kernel(tc, xT, w_words, w_scales, b, gate, offs, pos1, pos2,
                 for a in range(PASSES):
                     nc.tensor.matmul_mx(
                         out=acc,
-                        lhsT=w[h][s][:, (e - e0) * PASSES + a, :].bitcast(FP8X4),
+                        lhsT=w[e // 2][:, e % 2 * PASSES + a, h * P : (h + 1) * P].bitcast(FP8X4),
                         lhsT_scale=w_sc[:, e * PASSES + a, h * 32 : (h + 1) * 32].bitcast(U8),
                         rhs=g_words[a][:, slots].bitcast(FP8X4),
                         rhs_scale=g_scales[4 * a : P, slots],
@@ -129,13 +136,9 @@ def tile_routed_moe_kernel(tc, xT, w_words, w_scales, b, gate, offs, pos1, pos2,
             cast(0, c0, c1, nc.vector.tensor_copy)
         for c0, c1 in ((256, 512), (640, T)):
             cast(0, c0, c1, nc.scalar.copy)
-        cast(1, 0, 512, nc.scalar.copy)
-        cast(1, 512, T, nc.vector.tensor_copy)
-        cast(2, 0, 512, nc.scalar.copy)
-        cast(2, 512, 640, nc.vector.tensor_copy)
-        cast(2, 640, T, nc.scalar.copy)
-        cast(3, 0, 512, nc.scalar.copy)
-        cast(3, 512, T, nc.scalar.copy)
+        for a in range(1, PASSES):
+            for c0, c1 in CHUNKS:
+                cast(a, c0, c1, nc.scalar.copy)
 
         for a in range(PASSES - 1):
             quantise(a)
@@ -144,18 +147,29 @@ def tile_routed_moe_kernel(tc, xT, w_words, w_scales, b, gate, offs, pos1, pos2,
         for s, (e0, e1) in enumerate(GROUPS):
             gather_scales(e0, e1)
             gather_words(PASSES - 1, e0, e1)
-            multiply(0, s)
-        for s in range(len(GROUPS)):
-            multiply(1, s)
+            for h in range(HALVES):
+                multiply(h, s)
 
-        def combine(h, c0, c1):
-            for r, p in ((0, p1), (1, p2)):
-                nc.vector.tensor_tensor(
-                    t[h][r][:, c0:c1], y[h][:].indirect(p[:, c0 // 16 : c1 // 16]), g[h][r][:, c0:c1], MULT
-                )
-            nc.vector.tensor_add(res[h][:, c0:c1], t[h][0][:, c0:c1], t[h][1][:, c0:c1])
+        def weigh(h, r, c0, c1):
+            p = (p1, p2)[r]
+            nc.vector.tensor_tensor(
+                t[h][r][:, c0:c1], y[h][:].indirect(p[:, c0 // 16 : c1 // 16]), g[h][r][:, c0:c1], MULT
+            )
+
+        def store(h, c0, c1):
             nc.sync.dma_start(out=out[h * P : (h + 1) * P, c0:c1], in_=res[h][:, c0:c1])
 
-        combine(0, 0, T)
-        combine(1, 0, 512)
-        combine(1, 512, T)
+        weigh(0, 0, 0, T)
+        weigh(0, 1, 0, T)
+        for j, (c0, c1) in enumerate(CHUNKS):
+            total = banks[0][j][:, 0 : c1 - c0]
+            for r in range(2):
+                nc.tensor.matmul(total, ident[:], t[0][r][:, c0:c1], start=(r == 0), stop=(r == 1))
+            nc.scalar.copy(res[0][:, c0:c1], total)
+        store(0, 0, T)
+        weigh(1, 0, 0, T)
+        for c0, c1 in CHUNKS:
+            weigh(1, 1, c0, c1)
+        for c0, c1 in CHUNKS:
+            nc.vector.tensor_add(res[1][:, c0:c1], t[1][0][:, c0:c1], t[1][1][:, c0:c1])
+            store(1, c0, c1)

@@ -1,7 +1,6 @@
 from contextlib import ExitStack
 
 import concourse.mybir as mybir
-from concourse.masks import make_identity
 
 K, T, E, C, N = 2048, 768, 12, 128, 256
 FLOPS = 2 * K * N * E * C
@@ -22,6 +21,7 @@ HALVES = N // P
 WIDE = 2048
 GROUPS = ((0, 4), (4, 8), (8, 10), (10, 12))
 BANKS = 4
+WHOLE = 8
 CHUNKS = ((0, 512), (512, 768))
 
 
@@ -42,7 +42,8 @@ def tile_routed_moe_kernel(tc, xT, w_words, w_scales, b, gate, offs, pos1, pos2,
         scales = keep.tile([P, T], U8, name="scales", align_bytes=64)
         g_words = [keep.tile([P, E * C], U32, name=f"g_words{a}", align_bytes=64) for a in range(PASSES)]
         g_scales = keep.tile([P, E * C], U8, name="g_scales", align_bytes=64)
-        w = [keep.tile([P, 2 * PASSES, N], I32, name=f"w{v}", align_bytes=64) for v in range(E // 2)]
+        w = [keep.tile([P, 2 * PASSES, N], I32, name=f"w{v}", align_bytes=64) for v in range(WHOLE // 2)]
+        w_half = [[keep.tile([P, 2 * PASSES, P], I32, name=f"w{v}_{h}", align_bytes=64) for v in range(WHOLE // 2, E // 2)] for h in range(HALVES)]
         w_sc = keep.tile([P, E * PASSES, N // 4], I32, name="w_sc", align_bytes=64)
         y = [keep.tile([P, E * C], F32, name=f"y{h}") for h in range(HALVES)]
         g = [[keep.tile([P, T], F32, name=f"g{h}_{r}") for r in range(2)] for h in range(HALVES)]
@@ -50,9 +51,7 @@ def tile_routed_moe_kernel(tc, xT, w_words, w_scales, b, gate, offs, pos1, pos2,
         res = [keep.tile([P, T], F32, name=f"res{h}") for h in range(HALVES)]
         banks = [[psum.tile([P, 512], F32, name=f"bank{h}_{j}") for j in range(BANKS)] for h in range(HALVES)]
 
-        ident = keep.tile([P, P], F32, name="ident")
         nc.gpsimd.memset(scales[:], 0)
-        make_identity(nc, ident[:])
         nc.vector.memset(warm[:], 0.0)
         nc.vector.memset(w_sc[:], 0)
         for a in range(PASSES - 1):
@@ -63,31 +62,29 @@ def tile_routed_moe_kernel(tc, xT, w_words, w_scales, b, gate, offs, pos1, pos2,
         nc.sync.dma_start(out=raw[0][:, :, 0:512], in_=x_rows[0, :, :, 0:512])
         nc.sync.dma_start(out=raw[0][:, :, 512:T], in_=x_rows[0, :, :, 512:T])
         nc.sync.dma_start(lists[:], offs)
-        ws_rows = w_scales.rearrange("e a q n -> q (e a) n")
+        for a in range(1, PASSES):
+            nc.sync.dma_start(out=raw[a][:], in_=x_rows[a])
         w_rows = w_words.rearrange("e a p n r -> p (e a) (n r)")
 
-        def load_w_scales(q0, q1):
-            for q in range(q0, q1):
-                row = q // 4 * 32 + q % 4
-                nc.sync.dma_start(out=w_sc[row : row + 1], in_=ws_rows[q : q + 1].bitcast(I32))
+        def load_w(v, tile, n0, n1):
+            nc.sync.dma_start(out=tile, in_=w_rows[:, v * 2 * PASSES : (v + 1) * 2 * PASSES, 4 * n0 : 4 * n1].bitcast(I32))
 
-        def load_w(v):
-            nc.sync.dma_start(out=w[v][:], in_=w_rows[:, v * 2 * PASSES : (v + 1) * 2 * PASSES, :].bitcast(I32))
+        def load_gate(h):
+            for r in range(2):
+                nc.sync.dma_start(out=g[h][r][:], in_=gate[r, h * P : (h + 1) * P, :])
 
-        for c0, c1 in CHUNKS:
-            nc.sync.dma_start(out=raw[1][:, :, c0:c1], in_=x_rows[1, :, :, c0:c1])
-        load_w_scales(0, 2)
-        nc.sync.dma_start(out=raw[2][:], in_=x_rows[2])
-        load_w_scales(2, 4)
-        nc.sync.dma_start(out=raw[3][:], in_=x_rows[3])
-        for v in range(E // 2):
-            load_w_scales(4 + 3 * v, min(7 + 3 * v, 16))
-            load_w(v)
+        load_w(0, w[0][:], 0, N)
+        ws_rows = w_scales.rearrange("e a (q i) n -> i q (e a) n", i=4)
+        for i in range(4):
+            nc.sync.dma_start(out=w_sc[i:P:32], in_=ws_rows[i].bitcast(I32))
+        for v in range(1, WHOLE // 2):
+            load_w(v, w[v][:], 0, N)
         nc.sync.dma_start(p1[:], pos1)
         nc.sync.dma_start(p2[:], pos2)
         for h in range(HALVES):
-            for r in range(2):
-                nc.sync.dma_start(out=g[h][r][:], in_=gate[r, h * P : (h + 1) * P, :])
+            for v in range(WHOLE // 2, E // 2):
+                load_w(v, w_half[h][v - WHOLE // 2][:], h * P, (h + 1) * P)
+            load_gate(h)
         nc.scalar.dma_start(out=bias[:], in_=b.rearrange("(h p) e -> p h e", p=P))
 
         def cast(a, c0, c1, copy):
@@ -118,12 +115,16 @@ def tile_routed_moe_kernel(tc, xT, w_words, w_scales, b, gate, offs, pos1, pos2,
         def multiply(h, s):
             e0, e1 = GROUPS[s]
             for e in range(e0, e1):
+                if e < WHOLE:
+                    wt = w[e // 2][:, :, h * P : (h + 1) * P]
+                else:
+                    wt = w_half[h][(e - WHOLE) // 2][:]
                 acc = banks[h][e % BANKS][:, e // BANKS * C : (e // BANKS + 1) * C]
                 slots = slice(e * C, (e + 1) * C)
                 for a in range(PASSES):
                     nc.tensor.matmul_mx(
                         out=acc,
-                        lhsT=w[e // 2][:, e % 2 * PASSES + a, h * P : (h + 1) * P].bitcast(FP8X4),
+                        lhsT=wt[:, e % 2 * PASSES + a, :].bitcast(FP8X4),
                         lhsT_scale=w_sc[:, e * PASSES + a, h * 32 : (h + 1) * 32].bitcast(U8),
                         rhs=g_words[a][:, slots].bitcast(FP8X4),
                         rhs_scale=g_scales[4 * a : P, slots],
@@ -136,7 +137,9 @@ def tile_routed_moe_kernel(tc, xT, w_words, w_scales, b, gate, offs, pos1, pos2,
             cast(0, c0, c1, nc.vector.tensor_copy)
         for c0, c1 in ((256, 512), (640, T)):
             cast(0, c0, c1, nc.scalar.copy)
-        for a in range(1, PASSES):
+        cast(1, 0, 512, nc.scalar.copy)
+        cast(1, 512, T, nc.vector.tensor_copy)
+        for a in range(2, PASSES):
             for c0, c1 in CHUNKS:
                 cast(a, c0, c1, nc.scalar.copy)
 
@@ -147,8 +150,11 @@ def tile_routed_moe_kernel(tc, xT, w_words, w_scales, b, gate, offs, pos1, pos2,
         for s, (e0, e1) in enumerate(GROUPS):
             gather_scales(e0, e1)
             gather_words(PASSES - 1, e0, e1)
-            for h in range(HALVES):
+            for h in range(HALVES if e1 <= WHOLE else 1):
                 multiply(h, s)
+        for s, (e0, e1) in enumerate(GROUPS):
+            if e0 >= WHOLE:
+                multiply(1, s)
 
         def weigh(h, r, c0, c1):
             p = (p1, p2)[r]
@@ -161,11 +167,7 @@ def tile_routed_moe_kernel(tc, xT, w_words, w_scales, b, gate, offs, pos1, pos2,
 
         weigh(0, 0, 0, T)
         weigh(0, 1, 0, T)
-        for j, (c0, c1) in enumerate(CHUNKS):
-            total = banks[0][j][:, 0 : c1 - c0]
-            for r in range(2):
-                nc.tensor.matmul(total, ident[:], t[0][r][:, c0:c1], start=(r == 0), stop=(r == 1))
-            nc.scalar.copy(res[0][:, c0:c1], total)
+        nc.vector.tensor_add(res[0][:], t[0][0][:], t[0][1][:])
         store(0, 0, T)
         weigh(1, 0, 0, T)
         for c0, c1 in CHUNKS:

@@ -18,7 +18,7 @@ MULT = mybir.AluOpType.mult
 P = 128
 PASSES = K // 512
 HALVES = N // P
-WIDE = 2048
+WIDE = 1024
 GROUPS = ((0, 4), (4, 8), (8, 10), (10, 12))
 BANKS = 4
 WHOLE = 8
@@ -53,7 +53,7 @@ def tile_routed_moe_kernel(tc, xT, w_words, w_scales, b, gate, offs, pos1, pos2,
 
         nc.gpsimd.memset(scales[:], 0)
         nc.vector.memset(warm[:], 0.0)
-        nc.vector.memset(w_sc[:], 0)
+        nc.gpsimd.memset(w_sc[:], 0)
         for a in range(PASSES - 1):
             nc.vector.memset(words[a][:, T:WIDE], 0)
         nc.scalar.activation(warm[:], warm[:], SILU)
@@ -62,7 +62,9 @@ def tile_routed_moe_kernel(tc, xT, w_words, w_scales, b, gate, offs, pos1, pos2,
         nc.sync.dma_start(out=raw[0][:, :, 0:512], in_=x_rows[0, :, :, 0:512])
         nc.sync.dma_start(out=raw[0][:, :, 512:T], in_=x_rows[0, :, :, 512:T])
         nc.sync.dma_start(lists[:], offs)
-        for a in range(1, PASSES):
+        for c0, c1 in CHUNKS:
+            nc.sync.dma_start(out=raw[1][:, :, c0:c1], in_=x_rows[1, :, :, c0:c1])
+        for a in range(2, PASSES):
             nc.sync.dma_start(out=raw[a][:], in_=x_rows[a])
         w_rows = w_words.rearrange("e a p n r -> p (e a) (n r)")
 
@@ -137,15 +139,14 @@ def tile_routed_moe_kernel(tc, xT, w_words, w_scales, b, gate, offs, pos1, pos2,
             cast(0, c0, c1, nc.vector.tensor_copy)
         for c0, c1 in ((256, 512), (640, T)):
             cast(0, c0, c1, nc.scalar.copy)
-        cast(1, 0, 512, nc.scalar.copy)
-        cast(1, 512, T, nc.vector.tensor_copy)
-        for a in range(2, PASSES):
+        for a in range(1, PASSES):
             for c0, c1 in CHUNKS:
                 cast(a, c0, c1, nc.scalar.copy)
 
         for a in range(PASSES - 1):
             quantise(a)
-            gather_words(a, 0, E)
+            gather_words(a, 0, E // 2)
+            gather_words(a, E // 2, E)
         quantise(PASSES - 1)
         for s, (e0, e1) in enumerate(GROUPS):
             gather_scales(e0, e1)

@@ -16,13 +16,18 @@ SILU = mybir.ActivationFunctionType.Silu
 MULT = mybir.AluOpType.mult
 
 P = 128
-PASSES = K // 512
+PACK = 4
+PASSES = K // (P * PACK)
 HALVES = N // P
+LIST = 16
+
+CHUNKS = ((0, 512), (512, T))
 WIDE = 1024
-GROUPS = ((0, 4), (4, 8), (8, 10), (10, 12))
+LAST_GATHERS = ((0, 4), (4, 8), (8, 10), (10, 12))
+WHOLE_LOADS = ((0, 2), (2, 4), (4, 6), (6, 8))
+HALF_LOADS = (((8, 10), (10, 12)), ((8, 10), (10, 11), (11, 12)))
+WHOLE = WHOLE_LOADS[-1][1]
 BANKS = 4
-WHOLE = 8
-CHUNKS = ((0, 512), (512, 768))
 
 
 def tile_routed_moe_kernel(tc, xT, w_words, w_scales, b, gate, offs, pos1, pos2, out):
@@ -31,69 +36,74 @@ def tile_routed_moe_kernel(tc, xT, w_words, w_scales, b, gate, offs, pos1, pos2,
         keep = ctx.enter_context(tc.tile_pool(name="keep", bufs=1))
         psum = ctx.enter_context(tc.psum_pool(name="psum", bufs=1))
 
-        lists = keep.tile([P, E * C // 16], U16, name="lists")
-        p1 = keep.tile([P, T // 16], U16, name="p1")
-        p2 = keep.tile([P, T // 16], U16, name="p2")
+        slot_list = keep.tile([P, E * C // LIST], U16, name="slot_list")
+        pos_lists = [keep.tile([P, T // LIST], U16, name=f"pos_list{r}") for r in range(2)]
         bias = keep.tile([P, HALVES, E], F32, name="bias")
-        warm = keep.tile([P, 8], F32, name="warm")
-        raw = [keep.tile([P, 4, T], F32, name=f"raw{a}") for a in range(PASSES)]
-        pairs = [[keep.tile([P, c1 - c0, 4], BF16, name=f"pairs{a}_{c0}", align_bytes=64) for c0, c1 in CHUNKS] for a in range(PASSES)]
-        words = [keep.tile([P, WIDE if a < PASSES - 1 else T], I32, name=f"words{a}", align_bytes=64) for a in range(PASSES)]
+        table = keep.tile([P, 8], F32, name="table")
+        raw = [keep.tile([P, PACK, T], F32, name=f"raw{a}") for a in range(PASSES)]
+        grouped = [
+            [keep.tile([P, c1 - c0, PACK], BF16, name=f"grouped{a}_{c0}", align_bytes=64) for c0, c1 in CHUNKS]
+            for a in range(PASSES)
+        ]
+        words = [
+            keep.tile([P, WIDE if a < PASSES - 1 else T], I32, name=f"words{a}", align_bytes=64) for a in range(PASSES)
+        ]
         scales = keep.tile([P, T], U8, name="scales", align_bytes=64)
-        g_words = [keep.tile([P, E * C], U32, name=f"g_words{a}", align_bytes=64) for a in range(PASSES)]
-        g_scales = keep.tile([P, E * C], U8, name="g_scales", align_bytes=64)
-        w = [keep.tile([P, 2 * PASSES, N], I32, name=f"w{v}", align_bytes=64) for v in range(WHOLE // 2)]
-        w_half = [[keep.tile([P, 2 * PASSES, P], I32, name=f"w{v}_{h}", align_bytes=64) for v in range(WHOLE // 2, E // 2)] for h in range(HALVES)]
-        w_sc = keep.tile([P, E * PASSES, N // 4], I32, name="w_sc", align_bytes=64)
-        y = [keep.tile([P, E * C], F32, name=f"y{h}") for h in range(HALVES)]
-        g = [[keep.tile([P, T], F32, name=f"g{h}_{r}") for r in range(2)] for h in range(HALVES)]
-        t = [[keep.tile([P, T], F32, name=f"t{h}_{r}") for r in range(2)] for h in range(HALVES)]
-        res = [keep.tile([P, T], F32, name=f"res{h}") for h in range(HALVES)]
+        slot_words = [keep.tile([P, E * C], U32, name=f"slot_words{a}", align_bytes=64) for a in range(PASSES)]
+        slot_scales = keep.tile([P, E * C], U8, name="slot_scales", align_bytes=64)
+        w_scale_words = keep.tile([P, E * PASSES, N // 4], I32, name="w_scale_words", align_bytes=64)
+        slots = [keep.tile([P, E * C], F32, name=f"slots{h}") for h in range(HALVES)]
+        gates = [[keep.tile([P, T], F32, name=f"gate{h}_{r}") for r in range(2)] for h in range(HALVES)]
+        terms = [[keep.tile([P, T], F32, name=f"term{h}_{r}") for r in range(2)] for h in range(HALVES)]
+        total = [keep.tile([P, T], F32, name=f"total{h}") for h in range(HALVES)]
         banks = [[psum.tile([P, 512], F32, name=f"bank{h}_{j}") for j in range(BANKS)] for h in range(HALVES)]
 
         nc.gpsimd.memset(scales[:], 0)
-        nc.vector.memset(warm[:], 0.0)
-        nc.gpsimd.memset(w_sc[:], 0)
+        nc.gpsimd.memset(w_scale_words[:], 0)
+        nc.vector.memset(table[:], 0.0)
         for a in range(PASSES - 1):
             nc.vector.memset(words[a][:, T:WIDE], 0)
-        nc.scalar.activation(warm[:], warm[:], SILU)
+        nc.scalar.activation(table[:], table[:], SILU)
 
-        x_rows = xT.rearrange("(a p t) n -> a p t n", p=P, t=4)
-        nc.sync.dma_start(out=raw[0][:, :, 0:512], in_=x_rows[0, :, :, 0:512])
-        nc.sync.dma_start(out=raw[0][:, :, 512:T], in_=x_rows[0, :, :, 512:T])
-        nc.sync.dma_start(lists[:], offs)
-        for c0, c1 in CHUNKS:
-            nc.sync.dma_start(out=raw[1][:, :, c0:c1], in_=x_rows[1, :, :, c0:c1])
-        for a in range(2, PASSES):
+        x_rows = xT.rearrange("(a p t) c -> a p t c", p=P, t=PACK)
+        nc.sync.dma_start(out=raw[0][:], in_=x_rows[0])
+        nc.sync.dma_start(slot_list[:], offs)
+        for a in range(1, PASSES):
             nc.sync.dma_start(out=raw[a][:], in_=x_rows[a])
+
+        weights = [[None] * E for h in range(HALVES)]
         w_rows = w_words.rearrange("e a p n r -> p (e a) (n r)")
 
-        def load_w(v, tile, n0, n1):
-            nc.sync.dma_start(out=tile, in_=w_rows[:, v * 2 * PASSES : (v + 1) * 2 * PASSES, 4 * n0 : 4 * n1].bitcast(I32))
+        def load_weights(e0, e1, halves):
+            width = len(halves) * P
+            n0 = halves[0] * P
+            tile = keep.tile([P, (e1 - e0) * PASSES, width], I32, name=f"w{e0}_{n0}", align_bytes=64)
+            rows = w_rows[:, e0 * PASSES : e1 * PASSES, PACK * n0 : PACK * (n0 + width)]
+            nc.sync.dma_start(out=tile[:], in_=rows.bitcast(I32))
+            for e in range(e0, e1):
+                for j, h in enumerate(halves):
+                    weights[h][e] = tile[:, (e - e0) * PASSES : (e - e0 + 1) * PASSES, j * P : (j + 1) * P]
 
-        def load_gate(h):
-            for r in range(2):
-                nc.sync.dma_start(out=g[h][r][:], in_=gate[r, h * P : (h + 1) * P, :])
-
-        load_w(0, w[0][:], 0, N)
-        ws_rows = w_scales.rearrange("e a (q i) n -> i q (e a) n", i=4)
+        load_weights(*WHOLE_LOADS[0], (0, 1))
+        scale_rows = w_scales.rearrange("e a (q i) n -> i q (e a) n", i=4)
         for i in range(4):
-            nc.sync.dma_start(out=w_sc[i:P:32], in_=ws_rows[i].bitcast(I32))
-        for v in range(1, WHOLE // 2):
-            load_w(v, w[v][:], 0, N)
-        nc.sync.dma_start(p1[:], pos1)
-        nc.sync.dma_start(p2[:], pos2)
+            nc.sync.dma_start(out=w_scale_words[i:P:32], in_=scale_rows[i].bitcast(I32))
+        for e0, e1 in WHOLE_LOADS[1:]:
+            load_weights(e0, e1, (0, 1))
+        for r, pos in enumerate((pos1, pos2)):
+            nc.sync.dma_start(pos_lists[r][:], pos)
         for h in range(HALVES):
-            for v in range(WHOLE // 2, E // 2):
-                load_w(v, w_half[h][v - WHOLE // 2][:], h * P, (h + 1) * P)
-            load_gate(h)
+            for e0, e1 in HALF_LOADS[h]:
+                load_weights(e0, e1, (h,))
+            for r in range(2):
+                nc.sync.dma_start(out=gates[h][r][:], in_=gate[r, h * P : (h + 1) * P, :])
         nc.scalar.dma_start(out=bias[:], in_=b.rearrange("(h p) e -> p h e", p=P))
 
-        def cast(a, c0, c1, copy):
-            j = 0 if c0 < 512 else 1
-            base = CHUNKS[j][0]
+        def group(a, c0, c1, copy):
+            j = 0 if c0 < CHUNKS[0][1] else 1
+            first = CHUNKS[j][0]
             copy(
-                out=pairs[a][j][:, c0 - base : c1 - base, :].rearrange("p (c i) t -> p c t i", i=4),
+                out=grouped[a][j][:, c0 - first : c1 - first, :].rearrange("p (c i) t -> p c t i", i=4),
                 in_=raw[a][:, :, c0:c1].rearrange("p t (c i) -> p c t i", i=4),
             )
 
@@ -102,77 +112,72 @@ def tile_routed_moe_kernel(tc, xT, w_words, w_scales, b, gate, offs, pos1, pos2,
                 nc.vector.quantize_mx(
                     out=words[a][:, c0:c1].bitcast(FP8X4),
                     scales=scales[4 * a : P, c0:c1],
-                    in_=pairs[a][j][:].rearrange("p c t -> p (c t)"),
+                    in_=grouped[a][j][:].rearrange("p c t -> p (c t)"),
                 )
 
+        def columns(e0, e1):
+            return slot_list[:, e0 * C // LIST : e1 * C // LIST]
+
         def gather_words(a, e0, e1):
-            nc.vector.tensor_copy(
-                g_words[a][:, e0 * C : e1 * C],
-                words[a][:].bitcast(U32).indirect(lists[:, e0 * C // 16 : e1 * C // 16]),
-            )
+            window = words[a][:].bitcast(U32)
+            nc.vector.tensor_copy(slot_words[a][:, e0 * C : e1 * C], window.indirect(columns(e0, e1)))
 
         def gather_scales(e0, e1):
-            nc.vector.tensor_copy(g_scales[:, e0 * C : e1 * C], scales[:].indirect(lists[:, e0 * C // 16 : e1 * C // 16]))
+            nc.vector.tensor_copy(slot_scales[:, e0 * C : e1 * C], scales[:].indirect(columns(e0, e1)))
 
-        def multiply(h, s):
-            e0, e1 = GROUPS[s]
-            for e in range(e0, e1):
-                if e < WHOLE:
-                    wt = w[e // 2][:, :, h * P : (h + 1) * P]
-                else:
-                    wt = w_half[h][(e - WHOLE) // 2][:]
-                acc = banks[h][e % BANKS][:, e // BANKS * C : (e // BANKS + 1) * C]
-                slots = slice(e * C, (e + 1) * C)
-                for a in range(PASSES):
-                    nc.tensor.matmul_mx(
-                        out=acc,
-                        lhsT=wt[:, e % 2 * PASSES + a, :].bitcast(FP8X4),
-                        lhsT_scale=w_sc[:, e * PASSES + a, h * 32 : (h + 1) * 32].bitcast(U8),
-                        rhs=g_words[a][:, slots].bitcast(FP8X4),
-                        rhs_scale=g_scales[4 * a : P, slots],
-                        start=(a == 0),
-                        stop=(a == PASSES - 1),
-                    )
-                nc.scalar.activation(y[h][:, slots], acc, SILU, bias=bias[:, h, e : e + 1])
+        def multiply(h, e):
+            own = slice(e * C, (e + 1) * C)
+            acc = banks[h][e % BANKS][:, e // BANKS * C : (e // BANKS + 1) * C]
+            for a in range(PASSES):
+                nc.tensor.matmul_mx(
+                    out=acc,
+                    lhsT=weights[h][e][:, a, :].bitcast(FP8X4),
+                    lhsT_scale=w_scale_words[:, e * PASSES + a, h * P // 4 : (h + 1) * P // 4].bitcast(U8),
+                    rhs=slot_words[a][:, own].bitcast(FP8X4),
+                    rhs_scale=slot_scales[4 * a : P, own],
+                    start=(a == 0),
+                    stop=(a == PASSES - 1),
+                )
+            nc.scalar.activation(slots[h][:, own], acc, SILU, bias=bias[:, h, e : e + 1])
 
-        for c0, c1 in ((0, 256), (512, 640)):
-            cast(0, c0, c1, nc.vector.tensor_copy)
-        for c0, c1 in ((256, 512), (640, T)):
-            cast(0, c0, c1, nc.scalar.copy)
-        for a in range(1, PASSES):
+        for c0, c1 in ((0, 256), (512, 704)):
+            group(0, c0, c1, nc.vector.tensor_copy)
+        for c0, c1 in ((256, 512), (704, T)):
+            group(0, c0, c1, nc.scalar.copy)
+        group(1, *CHUNKS[0], nc.scalar.copy)
+        group(1, *CHUNKS[1], nc.vector.tensor_copy)
+        for a in range(2, PASSES):
             for c0, c1 in CHUNKS:
-                cast(a, c0, c1, nc.scalar.copy)
+                group(a, c0, c1, nc.scalar.copy)
 
         for a in range(PASSES - 1):
             quantise(a)
             gather_words(a, 0, E // 2)
             gather_words(a, E // 2, E)
         quantise(PASSES - 1)
-        for s, (e0, e1) in enumerate(GROUPS):
+        for e0, e1 in LAST_GATHERS:
             gather_scales(e0, e1)
             gather_words(PASSES - 1, e0, e1)
-            for h in range(HALVES if e1 <= WHOLE else 1):
-                multiply(h, s)
-        for s, (e0, e1) in enumerate(GROUPS):
-            if e0 >= WHOLE:
-                multiply(1, s)
+            for h in range(HALVES):
+                for e in range(e0, e1):
+                    if h == 0 or e < WHOLE:
+                        multiply(h, e)
+        for e in range(WHOLE, E):
+            multiply(1, e)
 
         def weigh(h, r, c0, c1):
-            p = (p1, p2)[r]
-            nc.vector.tensor_tensor(
-                t[h][r][:, c0:c1], y[h][:].indirect(p[:, c0 // 16 : c1 // 16]), g[h][r][:, c0:c1], MULT
-            )
+            offsets = pos_lists[r][:, c0 // LIST : c1 // LIST]
+            nc.vector.tensor_tensor(terms[h][r][:, c0:c1], slots[h][:].indirect(offsets), gates[h][r][:, c0:c1], MULT)
 
-        def store(h, c0, c1):
-            nc.sync.dma_start(out=out[h * P : (h + 1) * P, c0:c1], in_=res[h][:, c0:c1])
+        def finish(h, c0, c1):
+            nc.vector.tensor_add(total[h][:, c0:c1], terms[h][0][:, c0:c1], terms[h][1][:, c0:c1])
+            nc.sync.dma_start(out=out[h * P : (h + 1) * P, c0:c1], in_=total[h][:, c0:c1])
 
         weigh(0, 0, 0, T)
         weigh(0, 1, 0, T)
-        nc.vector.tensor_add(res[0][:], t[0][0][:], t[0][1][:])
-        store(0, 0, T)
+        finish(0, 0, T)
         weigh(1, 0, 0, T)
         for c0, c1 in CHUNKS:
             weigh(1, 1, c0, c1)
         for c0, c1 in CHUNKS:
-            nc.vector.tensor_add(res[1][:, c0:c1], t[1][0][:, c0:c1], t[1][1][:, c0:c1])
-            store(1, c0, c1)
+            finish(1, c0, c1)

from contextlib import ExitStack

import concourse.mybir as mybir

K, T, E, C, N = 2048, 768, 12, 128, 256
FLOPS = 2 * K * N * E * C

F32 = mybir.dt.float32
BF16 = mybir.dt.bfloat16
U32 = mybir.dt.uint32
I32 = mybir.dt.int32
U16 = mybir.dt.uint16
U8 = mybir.dt.uint8
FP8X4 = mybir.dt.float8_e4m3fn_x4
SILU = mybir.ActivationFunctionType.Silu
MULT = mybir.AluOpType.mult

P = 128
PACK = 4
PASSES = K // (P * PACK)
HALVES = N // P
LIST = 16

CHUNKS = ((0, 512), (512, T))
WIDE = 1024
LAST_GATHERS = ((0, 4), (4, 8), (8, 10), (10, 12))
WHOLE_LOADS = ((0, 2), (2, 4), (4, 6), (6, 8))
HALF_LOADS = (((8, 10), (10, 12)), ((8, 10), (10, 11), (11, 12)))
WHOLE = WHOLE_LOADS[-1][1]
BANKS = 4


def tile_routed_moe_kernel(tc, xT, w_words, w_scales, b, gate, offs, pos1, pos2, out):
    nc = tc.nc
    with ExitStack() as ctx:
        keep = ctx.enter_context(tc.tile_pool(name="keep", bufs=1))
        psum = ctx.enter_context(tc.psum_pool(name="psum", bufs=1))

        slot_list = keep.tile([P, E * C // LIST], U16, name="slot_list")
        pos_lists = [keep.tile([P, T // LIST], U16, name=f"pos_list{r}") for r in range(2)]
        bias = keep.tile([P, HALVES, E], F32, name="bias")
        table = keep.tile([P, 8], F32, name="table")
        raw = [keep.tile([P, PACK, T], F32, name=f"raw{a}") for a in range(PASSES)]
        grouped = [
            [keep.tile([P, c1 - c0, PACK], BF16, name=f"grouped{a}_{c0}", align_bytes=64) for c0, c1 in CHUNKS]
            for a in range(PASSES)
        ]
        words = [
            keep.tile([P, WIDE if a < PASSES - 1 else T], I32, name=f"words{a}", align_bytes=64) for a in range(PASSES)
        ]
        scales = keep.tile([P, T], U8, name="scales", align_bytes=64)
        slot_words = [keep.tile([P, E * C], U32, name=f"slot_words{a}", align_bytes=64) for a in range(PASSES)]
        slot_scales = keep.tile([P, E * C], U8, name="slot_scales", align_bytes=64)
        w_scale_words = keep.tile([P, E * PASSES, N // 4], I32, name="w_scale_words", align_bytes=64)
        slots = [keep.tile([P, E * C], F32, name=f"slots{h}") for h in range(HALVES)]
        gates = [[keep.tile([P, T], F32, name=f"gate{h}_{r}") for r in range(2)] for h in range(HALVES)]
        terms = [[keep.tile([P, T], F32, name=f"term{h}_{r}") for r in range(2)] for h in range(HALVES)]
        total = [keep.tile([P, T], F32, name=f"total{h}") for h in range(HALVES)]
        banks = [[psum.tile([P, 512], F32, name=f"bank{h}_{j}") for j in range(BANKS)] for h in range(HALVES)]

        nc.gpsimd.memset(scales[:], 0)
        nc.gpsimd.memset(w_scale_words[:], 0)
        nc.vector.memset(table[:], 0.0)
        for a in range(PASSES - 1):
            nc.vector.memset(words[a][:, T:WIDE], 0)
        nc.scalar.activation(table[:], table[:], SILU)

        x_rows = xT.rearrange("(a p t) c -> a p t c", p=P, t=PACK)
        nc.sync.dma_start(out=raw[0][:], in_=x_rows[0])
        nc.sync.dma_start(slot_list[:], offs)
        for a in range(1, PASSES):
            nc.sync.dma_start(out=raw[a][:], in_=x_rows[a])

        weights = [[None] * E for h in range(HALVES)]
        w_rows = w_words.rearrange("e a p n r -> p (e a) (n r)")

        def load_weights(e0, e1, halves):
            width = len(halves) * P
            n0 = halves[0] * P
            tile = keep.tile([P, (e1 - e0) * PASSES, width], I32, name=f"w{e0}_{n0}", align_bytes=64)
            rows = w_rows[:, e0 * PASSES : e1 * PASSES, PACK * n0 : PACK * (n0 + width)]
            nc.sync.dma_start(out=tile[:], in_=rows.bitcast(I32))
            for e in range(e0, e1):
                for j, h in enumerate(halves):
                    weights[h][e] = tile[:, (e - e0) * PASSES : (e - e0 + 1) * PASSES, j * P : (j + 1) * P]

        load_weights(*WHOLE_LOADS[0], (0, 1))
        scale_rows = w_scales.rearrange("e a (q i) n -> i q (e a) n", i=4)
        for i in range(4):
            nc.sync.dma_start(out=w_scale_words[i:P:32], in_=scale_rows[i].bitcast(I32))
        for e0, e1 in WHOLE_LOADS[1:]:
            load_weights(e0, e1, (0, 1))
        for r, pos in enumerate((pos1, pos2)):
            nc.sync.dma_start(pos_lists[r][:], pos)
        for h in range(HALVES):
            for e0, e1 in HALF_LOADS[h]:
                load_weights(e0, e1, (h,))
            for r in range(2):
                nc.sync.dma_start(out=gates[h][r][:], in_=gate[r, h * P : (h + 1) * P, :])
        nc.scalar.dma_start(out=bias[:], in_=b.rearrange("(h p) e -> p h e", p=P))

        def group(a, c0, c1, copy):
            j = 0 if c0 < CHUNKS[0][1] else 1
            first = CHUNKS[j][0]
            copy(
                out=grouped[a][j][:, c0 - first : c1 - first, :].rearrange("p (c i) t -> p c t i", i=4),
                in_=raw[a][:, :, c0:c1].rearrange("p t (c i) -> p c t i", i=4),
            )

        def quantise(a):
            for j, (c0, c1) in enumerate(CHUNKS):
                nc.vector.quantize_mx(
                    out=words[a][:, c0:c1].bitcast(FP8X4),
                    scales=scales[4 * a : P, c0:c1],
                    in_=grouped[a][j][:].rearrange("p c t -> p (c t)"),
                )

        def columns(e0, e1):
            return slot_list[:, e0 * C // LIST : e1 * C // LIST]

        def gather_words(a, e0, e1):
            window = words[a][:].bitcast(U32)
            nc.vector.tensor_copy(slot_words[a][:, e0 * C : e1 * C], window.indirect(columns(e0, e1)))

        def gather_scales(e0, e1):
            nc.vector.tensor_copy(slot_scales[:, e0 * C : e1 * C], scales[:].indirect(columns(e0, e1)))

        def multiply(h, e):
            own = slice(e * C, (e + 1) * C)
            acc = banks[h][e % BANKS][:, e // BANKS * C : (e // BANKS + 1) * C]
            for a in range(PASSES):
                nc.tensor.matmul_mx(
                    out=acc,
                    lhsT=weights[h][e][:, a, :].bitcast(FP8X4),
                    lhsT_scale=w_scale_words[:, e * PASSES + a, h * P // 4 : (h + 1) * P // 4].bitcast(U8),
                    rhs=slot_words[a][:, own].bitcast(FP8X4),
                    rhs_scale=slot_scales[4 * a : P, own],
                    start=(a == 0),
                    stop=(a == PASSES - 1),
                )
            nc.scalar.activation(slots[h][:, own], acc, SILU, bias=bias[:, h, e : e + 1])

        for c0, c1 in ((0, 256), (512, 704)):
            group(0, c0, c1, nc.vector.tensor_copy)
        for c0, c1 in ((256, 512), (704, T)):
            group(0, c0, c1, nc.scalar.copy)
        group(1, *CHUNKS[0], nc.scalar.copy)
        group(1, *CHUNKS[1], nc.vector.tensor_copy)
        for a in range(2, PASSES):
            for c0, c1 in CHUNKS:
                group(a, c0, c1, nc.scalar.copy)

        for a in range(PASSES - 1):
            quantise(a)
            gather_words(a, 0, E // 2)
            gather_words(a, E // 2, E)
        quantise(PASSES - 1)
        for e0, e1 in LAST_GATHERS:
            gather_scales(e0, e1)
            gather_words(PASSES - 1, e0, e1)
            for h in range(HALVES):
                for e in range(e0, e1):
                    if h == 0 or e < WHOLE:
                        multiply(h, e)
        for e in range(WHOLE, E):
            multiply(1, e)

        def weigh(h, r, c0, c1):
            offsets = pos_lists[r][:, c0 // LIST : c1 // LIST]
            nc.vector.tensor_tensor(terms[h][r][:, c0:c1], slots[h][:].indirect(offsets), gates[h][r][:, c0:c1], MULT)

        def finish(h, c0, c1):
            nc.vector.tensor_add(total[h][:, c0:c1], terms[h][0][:, c0:c1], terms[h][1][:, c0:c1])
            nc.sync.dma_start(out=out[h * P : (h + 1) * P, c0:c1], in_=total[h][:, c0:c1])

        weigh(0, 0, 0, T)
        weigh(0, 1, 0, T)
        finish(0, 0, T)
        weigh(1, 0, 0, T)
        for c0, c1 in CHUNKS:
            weigh(1, 1, c0, c1)
        for c0, c1 in CHUNKS:
            finish(1, c0, c1)
